import numpy as np
import ml_dtypes


def mxq(x, axis, fmt="e4m3"):
    dtype, down = {"e4m3": (ml_dtypes.float8_e4m3fn, 7), "e5m2": (ml_dtypes.float8_e5m2, 14)}[fmt]
    v = np.moveaxis(np.asarray(x, np.float32).astype(ml_dtypes.bfloat16).astype(np.float64), axis, -1)
    blocks = v.reshape(v.shape[:-1] + (-1, 32))
    amax = np.abs(blocks).max(-1, keepdims=True)
    byte = np.maximum(np.where(amax > 0, np.frexp(amax)[1] - 1 + 127, 0) - down, 1)
    scale = np.exp2(byte - 127.0)
    codes = (blocks / scale).astype(np.float32).astype(dtype).astype(np.float64)
    return np.moveaxis((codes * scale).reshape(v.shape), -1, axis)


WIDE = False


def mx_kscale(k):
    if not WIDE:
        return np.ones(k)
    levels = np.array([10, -10, 5, -5, 0])
    if k % 512:
        return np.exp2(np.random.permutation(np.resize(levels, k // 32))).repeat(32)
    a = np.empty((k // 512, 16))
    for p in range(k // 512):
        a[p, :8] = np.random.permutation(np.resize(levels, 8))
        for g in range(8):
            far = levels[np.abs(levels - a[p, g]) >= 10]
            a[p, g + 8] = far[np.random.randint(len(far))]
    return np.exp2(a.ravel()).repeat(32)


def f64(x):
    return np.asarray(x).astype(np.float64)


def striped(idx):
    return np.tile(np.asarray(idx).reshape(-1, 16).T, (8, 1)).astype(np.uint16)


def unstriped(offs):
    return offs[:16].T.reshape(-1).astype(np.int64)


E2M1 = np.array([0.0, 0.5, 1.0, 1.5, 2.0, 3.0, 4.0, 6.0, -0.0, -0.5, -1.0, -1.5, -2.0, -3.0, -4.0, -6.0])


def pack_weight(w, fmt):
    k, n = w.shape
    w = f64(np.asarray(w, np.float32).astype(ml_dtypes.bfloat16)).reshape(k // 32, 32, n)
    amax = np.abs(w).max(1)
    if fmt == "e4m3":
        byte = np.frexp(amax)[1] - 1 + 127 - 7
    else:
        mant, ex = np.frexp(amax / 6.0)
        byte = np.where(mant > 0.5, ex, ex - 1) + 127
    byte = np.clip(np.where(amax > 0, byte, 1), 1, 254)
    scaled = (w * np.exp2(127.0 - byte)[:, None, :]).reshape(k, n).astype(np.float32)
    by_word = np.ascontiguousarray(scaled.reshape(k // 512, 128, 4, n).transpose(0, 1, 3, 2))
    if fmt == "e4m3":
        words = by_word.astype(ml_dtypes.float8_e4m3fn).view(np.uint8)
    else:
        c = by_word.astype(ml_dtypes.float4_e2m1fn).view(np.uint8) & 0xF
        words = (c[..., 0::2] | (c[..., 1::2] << 4)).reshape(k // 512, 128, 2 * n)
    return np.ascontiguousarray(words), np.ascontiguousarray(byte.astype(np.uint8).reshape(k // 512, 16, n))


def unpack_weight(words, scales, fmt):
    g, _, n = scales.shape
    words = np.ascontiguousarray(words).reshape(g, 128, n, -1)
    if fmt == "e4m3":
        vals = words.view(ml_dtypes.float8_e4m3fn).astype(np.float64)
    else:
        nib = np.empty((g, 128, n, 4), np.uint8)
        nib[..., 0::2] = words & 0xF
        nib[..., 1::2] = words >> 4
        vals = E2M1[nib]
    vals = vals * np.repeat(np.exp2(scales.astype(np.float64) - 127.0), 8, axis=1)[..., None]
    return vals.transpose(0, 1, 3, 2).reshape(g * 512, n)


B, N, T, D, NQ = 1, 512, 2048, 512, 256


def setup_inputs():
    n = np.random.standard_normal
    idx = np.random.permutation(T)[:B * N]
    s = mx_kscale(D)[:, None]
    kp = pack_weight(n((D, T)) / s, "e4m3")
    return {
        "qT": (n((B, D, NQ)) * s * (1.00 / np.sqrt(D))).astype(np.float32),
        "k_words": kp[0],
        "k_scales": kp[1],
        "offs": striped(idx),
    }


def reference(qT, k_words, k_scales, offs):
    idx = unstriped(offs)
    pick = lambda x, which: x[:, which].reshape(x.shape[0], B, -1).transpose(1, 0, 2)
    k = unpack_weight(k_words, k_scales, "e4m3")
    kg = pick(k, idx)
    qq = mxq(f64(qT), 1, "e4m3")
    a = qq.transpose(0, 2, 1) @ kg
    m = np.max(a, axis=-1, keepdims=True)
    e = np.exp(a - m)
    l = np.sum(e, axis=-1, keepdims=True)
    y = e / l
    return y

@@ -1,0 +1,119 @@
+from contextlib import ExitStack
+
+import concourse.mybir as mybir
+
+NQ, D, T, N = 256, 512, 2048, 512
+FLOPS = 2 * NQ * D * N
+
+F32 = mybir.dt.float32
+BF16 = mybir.dt.bfloat16
+I32 = mybir.dt.int32
+U32 = mybir.dt.uint32
+U16 = mybir.dt.uint16
+U8 = mybir.dt.uint8
+FP8X4 = mybir.dt.float8_e4m3fn_x4
+ALU = mybir.AluOpType
+ACT = mybir.ActivationFunctionType
+AXIS = mybir.AxisListType
+
+P = 128
+PACK = 4
+HALF = N // 2
+LIST_COLS = N // 16
+V_COLS = 320
+
+
+def tile_attend_wts_topk_kernel(tc, qT, k_words, k_scales, offs, out):
+    nc = tc.nc
+    with ExitStack() as ctx:
+        sb = ctx.enter_context(tc.tile_pool(name="sb", bufs=1))
+        psum = ctx.enter_context(tc.psum_pool(name="psum", bufs=1))
+
+        offsets = sb.tile([P, LIST_COLS], U16, name="offsets")
+        pool_scales = sb.tile([P, T], U8, name="pool_scales", align_bytes=64)
+        pool_words = sb.tile([P, T], I32, name="pool_words", align_bytes=64)
+        q_rows = qT[0].rearrange("(p j) w -> p j w", j=PACK)
+        widths = [NQ]
+        q_raw = [sb.tile([P, PACK, w], F32, name=f"q_raw{i}") for i, w in enumerate(widths)]
+
+        nc.vector.memset(pool_scales[:].bitcast(I32), 0)
+        nc.sync.dma_start(offsets[:], offs)
+        nc.sync.dma_start(q_raw[0][:], q_rows[:, :, 0 : widths[0]])
+        scale_rows = k_scales[0].bitcast(I32).rearrange("(g r) w -> r g w", r=4)
+        for r in range(4):
+            nc.sync.dma_start(pool_scales[:].bitcast(I32)[r:P:32, :], scale_rows[r])
+        nc.sync.dma_start(pool_words[:], k_words[0].rearrange("p t r -> p (t r)").bitcast(I32))
+
+        def quantize_queries(i, cast):
+            w = widths[i]
+            q_bf = sb.tile([P, w, PACK], BF16, name=f"q_bf{i}", align_bytes=64)
+            codes = sb.tile([P, w], U32, name=f"q_codes{i}", align_bytes=64)
+            scales = sb.tile([P, w], U8, name=f"q_scales{i}", align_bytes=64)
+            cast(
+                q_bf[:].rearrange("p (c i) j -> p c j i", i=4),
+                q_raw[i][:].rearrange("p j (c i) -> p c j i", i=4),
+            )
+            nc.vector.quantize_mx(
+                out=codes[:].bitcast(FP8X4),
+                scales=scales[:],
+                in_=q_bf[:].rearrange("p w j -> p (w j)"),
+            )
+            return [(codes[:, c : c + P], scales[:, c : c + P]) for c in range(0, w, P)]
+
+        q_mx = quantize_queries(0, nc.vector.tensor_copy)
+
+        key_scales = sb.tile([P, N], U8, name="key_scales", align_bytes=64)
+        nc.vector.tensor_copy(key_scales[:], pool_scales[:].indirect(offsets[:]))
+        key_words = sb.tile([P, N], U32, name="key_words", align_bytes=64)
+
+        def scores(t, cols, name):
+            bank = psum.tile([P, cols.stop - cols.start], F32, name=name)
+            nc.tensor.matmul_mx(
+                out=bank[:],
+                lhsT=q_mx[t][0].bitcast(FP8X4),
+                lhsT_scale=q_mx[t][1],
+                rhs=key_words[:, cols].bitcast(FP8X4),
+                rhs_scale=key_scales[:, cols],
+                start=True,
+                stop=True,
+            )
+            return bank
+
+        banks = {}
+        for h in range(2):
+            cols = slice(h * HALF, (h + 1) * HALF)
+            list_cols = slice(h * LIST_COLS // 2, (h + 1) * LIST_COLS // 2)
+            nc.vector.tensor_copy(key_words[:, cols], pool_words[:].bitcast(U32).indirect(offsets[:, list_cols]))
+            for t in range(2):
+                banks[t, h] = scores(t, cols, f"bank{t}{h}")
+
+        neg_a = [sb.tile([P, N], F32, name=f"neg_a{t}") for t in range(2)]
+        neg_m = {}
+        for h in range(2):
+            for t in range(2):
+                neg_m[t, h] = sb.tile([P, 1], F32, name=f"neg_m{t}{h}")
+                nc.vector.tensor_scalar(
+                    neg_a[t][:, h * HALF : (h + 1) * HALF],
+                    banks[t, h][:],
+                    -1.0,
+                    neg_m[t, 0][:] if h else None,
+                    ALU.mult,
+                    ALU.min,
+                    accum_out=neg_m[t, h][:],
+                )
+
+        for t in range(2):
+            e = sb.tile([P, N], F32, name=f"e{t}")
+            row_sum = sb.tile([P, 1], F32, name=f"row_sum{t}")
+            inv_sum = sb.tile([P, 1], F32, name=f"inv_sum{t}")
+            rows = slice(t * P, (t + 1) * P)
+            nc.scalar.activation(e[:], neg_a[t][:], ACT.Exp, bias=neg_m[t, 1][:], scale=-1.0, accum_out=row_sum[:])
+            nc.vector.reciprocal(inv_sum[:], row_sum[:])
+            for i, (c0, c1, on_scalar) in enumerate([[(0, 256, False), (256, 512, False)], [(0, 320, False), (320, 512, True)]][t]):
+                y = sb.tile([P, c1 - c0], F32, name=f"y{t}{i}")
+                if on_scalar:
+                    nc.scalar.activation(y[:], e[:, c0:c1], ACT.Copy, scale=inv_sum[:])
+                    nc.scalar.dma_start(out[0, rows, c0:c1], y[:])
+                else:
+                    nc.vector.tensor_scalar(y[:], e[:, c0:c1], inv_sum[:], None, ALU.mult)
+                    nc.sync.dma_start(out[0, rows, c0:c1], y[:])

@@ -37,8 +37,8 @@ def tile_attend_wts_topk_kernel(tc, qT, k_words, k_scales, offs, out):
         q_raw = [sb.tile([P, PACK, w], F32, name=f"q_raw{i}") for i, w in enumerate(widths)]
 
         nc.vector.memset(pool_scales[:].bitcast(I32), 0)
-        nc.sync.dma_start(offsets[:], offs)
         nc.sync.dma_start(q_raw[0][:], q_rows[:, :, 0 : widths[0]])
+        nc.sync.dma_start(offsets[:], offs)
         scale_rows = k_scales[0].bitcast(I32).rearrange("(g r) w -> r g w", r=4)
         for r in range(4):
             nc.sync.dma_start(pool_scales[:].bitcast(I32)[r:P:32, :], scale_rows[r])
@@ -49,10 +49,11 @@ def tile_attend_wts_topk_kernel(tc, qT, k_words, k_scales, offs, out):
             q_bf = sb.tile([P, w, PACK], BF16, name=f"q_bf{i}", align_bytes=64)
             codes = sb.tile([P, w], U32, name=f"q_codes{i}", align_bytes=64)
             scales = sb.tile([P, w], U8, name=f"q_scales{i}", align_bytes=64)
-            cast(
-                q_bf[:].rearrange("p (c i) j -> p c j i", i=4),
-                q_raw[i][:].rearrange("p j (c i) -> p c j i", i=4),
-            )
+            for c, cast in ((0, nc.vector.tensor_copy), (P, nc.scalar.copy)):
+                cast(
+                    q_bf[:, c : c + P, :].rearrange("p (c i) j -> p c j i", i=4),
+                    q_raw[i][:, :, c : c + P].rearrange("p j (c i) -> p c j i", i=4),
+                )
             nc.vector.quantize_mx(
                 out=codes[:].bitcast(FP8X4),
                 scales=scales[:],

@@ -36,12 +36,11 @@ def tile_attend_wts_topk_kernel(tc, qT, k_words, k_scales, offs, out):
         widths = [NQ]
         q_raw = [sb.tile([P, PACK, w], F32, name=f"q_raw{i}") for i, w in enumerate(widths)]
 
-        nc.vector.memset(pool_scales[:].bitcast(I32), 0)
-        nc.sync.dma_start(q_raw[0][:], q_rows[:, :, 0 : widths[0]])
+        for p0, p1 in ((0, 16), (32, 64), (64, P)):
+            nc.vector.memset(pool_scales[:].bitcast(I32)[p0:p1, :], 0)
+        nc.scalar.dma_start(pool_scales[:].bitcast(I32)[16:32, :], k_scales[0].bitcast(I32))
         nc.sync.dma_start(offsets[:], offs)
-        scale_rows = k_scales[0].bitcast(I32).rearrange("(g r) w -> r g w", r=4)
-        for r in range(4):
-            nc.sync.dma_start(pool_scales[:].bitcast(I32)[r:P:32, :], scale_rows[r])
+        nc.sync.dma_start(q_raw[0][:], q_rows)
         nc.sync.dma_start(pool_words[:], k_words[0].rearrange("p t r -> p (t r)").bitcast(I32))
 
         def quantize_queries(i, cast):
@@ -49,22 +48,28 @@ def tile_attend_wts_topk_kernel(tc, qT, k_words, k_scales, offs, out):
             q_bf = sb.tile([P, w, PACK], BF16, name=f"q_bf{i}", align_bytes=64)
             codes = sb.tile([P, w], U32, name=f"q_codes{i}", align_bytes=64)
             scales = sb.tile([P, w], U8, name=f"q_scales{i}", align_bytes=64)
-            for c, cast in ((0, nc.vector.tensor_copy), (P, nc.scalar.copy)):
+            for c, cast in ((0, nc.vector.tensor_copy), (P, nc.vector.tensor_copy)):
                 cast(
                     q_bf[:, c : c + P, :].rearrange("p (c i) j -> p c j i", i=4),
                     q_raw[i][:, :, c : c + P].rearrange("p j (c i) -> p c j i", i=4),
                 )
-            nc.vector.quantize_mx(
-                out=codes[:].bitcast(FP8X4),
-                scales=scales[:],
-                in_=q_bf[:].rearrange("p w j -> p (w j)"),
-            )
+            for c in (0, P):
+                nc.vector.quantize_mx(
+                    out=codes[:, c : c + P].bitcast(FP8X4),
+                    scales=scales[:, c : c + P],
+                    in_=q_bf[:, c : c + P, :].rearrange("p w j -> p (w j)"),
+                )
             return [(codes[:, c : c + P], scales[:, c : c + P]) for c in range(0, w, P)]
 
-        q_mx = quantize_queries(0, nc.vector.tensor_copy)
-
+        spread_scales = sb.tile([P, N], U8, name="spread_scales", align_bytes=64)
+        nc.vector.tensor_copy(spread_scales[:], pool_scales[:].indirect(offsets[:]))
         key_scales = sb.tile([P, N], U8, name="key_scales", align_bytes=64)
-        nc.vector.tensor_copy(key_scales[:], pool_scales[:].indirect(offsets[:]))
+        nc.vector.memset(key_scales[:].bitcast(I32), 0)
+        for r in range(4):
+            queue = nc.scalar if r % 2 else nc.sync
+            queue.dma_start(key_scales[:].bitcast(I32)[r:P:32, :], spread_scales[:].bitcast(I32)[16 + r : 32 : 4, :])
+
+        q_mx = quantize_queries(0, nc.vector.tensor_copy)
         key_words = sb.tile([P, N], U32, name="key_words", align_bytes=64)
 
         def scores(t, cols, name):

@@ -20,7 +20,7 @@ P = 128
 PACK = 4
 HALF = N // 2
 LIST_COLS = N // 16
-V_COLS = 320
+ROW0 = 16
 
 
 def tile_attend_wts_topk_kernel(tc, qT, k_words, k_scales, offs, out):
@@ -33,87 +33,72 @@ def tile_attend_wts_topk_kernel(tc, qT, k_words, k_scales, offs, out):
         pool_scales = sb.tile([P, T], U8, name="pool_scales", align_bytes=64)
         pool_words = sb.tile([P, T], I32, name="pool_words", align_bytes=64)
         q_rows = qT[0].rearrange("(p j) w -> p j w", j=PACK)
-        widths = [NQ]
-        q_raw = [sb.tile([P, PACK, w], F32, name=f"q_raw{i}") for i, w in enumerate(widths)]
+        words_hbm = k_words[0].rearrange("p t r -> p (t r)").bitcast(I32)
+        q_raw = {(t, j): sb.tile([P, n, P], F32, name=f"q_raw{t}{j}", tag=f"q_raw{t}{j}", align_bytes=64) for t, j, n in ((0, 0, 2), (0, 2, 2), (1, 0, PACK))}
+        q_bf = [sb.tile([P, P, PACK], BF16, name=f"q_bf{t}", align_bytes=64) for t in range(2)]
+        q_codes = [sb.tile([P, P], U32, name=f"q_codes{t}", align_bytes=64) for t in range(2)]
+        q_scales = [sb.tile([P, P], U8, name=f"q_scales{t}", align_bytes=64) for t in range(2)]
 
-        for p0, p1 in ((0, 16), (32, 64), (64, P)):
+        for p0, p1 in ((0, ROW0), (32, 64), (64, P)):
             nc.vector.memset(pool_scales[:].bitcast(I32)[p0:p1, :], 0)
-        nc.scalar.dma_start(pool_scales[:].bitcast(I32)[16:32, :], k_scales[0].bitcast(I32))
+        nc.scalar.dma_start(pool_scales[:].bitcast(I32)[ROW0:32, :], k_scales[0].bitcast(I32))
         nc.sync.dma_start(offsets[:], offs)
-        nc.sync.dma_start(q_raw[0][:], q_rows)
-        nc.sync.dma_start(pool_words[:], k_words[0].rearrange("p t r -> p (t r)").bitcast(I32))
+        nc.sync.dma_start(q_raw[0, 0][:], q_rows[:, 0:2, 0:P])
+        nc.sync.dma_start(pool_words[:], words_hbm)
+        nc.sync.dma_start(q_raw[0, 2][:], q_rows[:, 2:PACK, 0:P])
+        nc.sync.dma_start(q_raw[1, 0][:], q_rows[:, :, P:NQ])
 
-        def quantize_queries(i, cast):
-            w = widths[i]
-            q_bf = sb.tile([P, w, PACK], BF16, name=f"q_bf{i}", align_bytes=64)
-            codes = sb.tile([P, w], U32, name=f"q_codes{i}", align_bytes=64)
-            scales = sb.tile([P, w], U8, name=f"q_scales{i}", align_bytes=64)
-            for c, cast in ((0, nc.vector.tensor_copy), (P, nc.vector.tensor_copy)):
-                cast(
-                    q_bf[:, c : c + P, :].rearrange("p (c i) j -> p c j i", i=4),
-                    q_raw[i][:, :, c : c + P].rearrange("p j (c i) -> p c j i", i=4),
-                )
-            for c in (0, P):
-                nc.vector.quantize_mx(
-                    out=codes[:, c : c + P].bitcast(FP8X4),
-                    scales=scales[:, c : c + P],
-                    in_=q_bf[:, c : c + P, :].rearrange("p w j -> p (w j)"),
-                )
-            return [(codes[:, c : c + P], scales[:, c : c + P]) for c in range(0, w, P)]
+        def cast(t, j):
+            raw = q_raw[t, j]
+            nc.scalar.copy(
+                q_bf[t][:, :, j : j + raw.shape[1]].rearrange("p (c i) j -> p c j i", i=4),
+                raw[:].rearrange("p j (c i) -> p c j i", i=4),
+            )
 
-        spread_scales = sb.tile([P, N], U8, name="spread_scales", align_bytes=64)
-        nc.vector.tensor_copy(spread_scales[:], pool_scales[:].indirect(offsets[:]))
-        key_scales = sb.tile([P, N], U8, name="key_scales", align_bytes=64)
-        nc.vector.memset(key_scales[:].bitcast(I32), 0)
+        def quantize(t):
+            nc.vector.quantize_mx(
+                out=q_codes[t][:].bitcast(FP8X4),
+                scales=q_scales[t][:],
+                in_=q_bf[t][:].rearrange("p w j -> p (w j)"),
+            )
+
+        cast(0, 0)
+        picked_scales = sb.tile([P, N], U8, name="picked_scales", align_bytes=64)
+        nc.vector.tensor_copy(picked_scales[:], pool_scales[:].indirect(offsets[:]))
+        key_scales = sb.tile([P, N], U8, name="key_scales", tag="q_raw00", align_bytes=64)
+        nc.gpsimd.memset(key_scales[:].bitcast(I32), 0)
         for r in range(4):
             queue = nc.scalar if r % 2 else nc.sync
-            queue.dma_start(key_scales[:].bitcast(I32)[r:P:32, :], spread_scales[:].bitcast(I32)[16 + r : 32 : 4, :])
+            queue.dma_start(key_scales[:].bitcast(I32)[r:P:32, :], picked_scales[:].bitcast(I32)[ROW0 + r : 32 : 4, :])
+        cast(0, 2)
+        cast(1, 0)
 
-        q_mx = quantize_queries(0, nc.vector.tensor_copy)
         key_words = sb.tile([P, N], U32, name="key_words", align_bytes=64)
+        nc.vector.tensor_copy(key_words[:], pool_words[:].bitcast(U32).indirect(offsets[:]))
+        quantize(0)
+        quantize(1)
 
-        def scores(t, cols, name):
-            bank = psum.tile([P, cols.stop - cols.start], F32, name=name)
-            nc.tensor.matmul_mx(
-                out=bank[:],
-                lhsT=q_mx[t][0].bitcast(FP8X4),
-                lhsT_scale=q_mx[t][1],
-                rhs=key_words[:, cols].bitcast(FP8X4),
-                rhs_scale=key_scales[:, cols],
-                start=True,
-                stop=True,
-            )
-            return bank
-
-        banks = {}
-        for h in range(2):
-            cols = slice(h * HALF, (h + 1) * HALF)
-            list_cols = slice(h * LIST_COLS // 2, (h + 1) * LIST_COLS // 2)
-            nc.vector.tensor_copy(key_words[:, cols], pool_words[:].bitcast(U32).indirect(offsets[:, list_cols]))
-            for t in range(2):
-                banks[t, h] = scores(t, cols, f"bank{t}{h}")
-
-        neg_a = [sb.tile([P, N], F32, name=f"neg_a{t}") for t in range(2)]
-        neg_m = {}
-        for h in range(2):
-            for t in range(2):
-                neg_m[t, h] = sb.tile([P, 1], F32, name=f"neg_m{t}{h}")
-                nc.vector.tensor_scalar(
-                    neg_a[t][:, h * HALF : (h + 1) * HALF],
-                    banks[t, h][:],
-                    -1.0,
-                    neg_m[t, 0][:] if h else None,
-                    ALU.mult,
-                    ALU.min,
-                    accum_out=neg_m[t, h][:],
+        banks = [psum.tile([P, N], F32, name=f"bank{t}") for t in range(2)]
+        neg_m = [sb.tile([P, 1], F32, name=f"neg_m{t}") for t in range(2)]
+        for t, pieces in enumerate(((0, N), (0, N))):
+            for c0, c1 in zip(pieces, pieces[1:]):
+                nc.tensor.matmul_mx(
+                    out=banks[t][:, c0:c1],
+                    lhsT=q_codes[t][:].bitcast(FP8X4),
+                    lhsT_scale=q_scales[t][:],
+                    rhs=key_words[:, c0:c1].bitcast(FP8X4),
+                    rhs_scale=key_scales[:, c0:c1],
+                    start=True,
+                    stop=True,
                 )
+            nc.vector.tensor_reduce(neg_m[t][:], banks[t][:], AXIS.X, ALU.max, negate=True)
 
         for t in range(2):
             e = sb.tile([P, N], F32, name=f"e{t}")
             row_sum = sb.tile([P, 1], F32, name=f"row_sum{t}")
             inv_sum = sb.tile([P, 1], F32, name=f"inv_sum{t}")
             rows = slice(t * P, (t + 1) * P)
-            nc.scalar.activation(e[:], neg_a[t][:], ACT.Exp, bias=neg_m[t, 1][:], scale=-1.0, accum_out=row_sum[:])
+            nc.scalar.activation(e[:], banks[t][:], ACT.Exp, bias=neg_m[t][:], accum_out=row_sum[:])
             nc.vector.reciprocal(inv_sum[:], row_sum[:])
             for i, (c0, c1, on_scalar) in enumerate([[(0, 256, False), (256, 512, False)], [(0, 320, False), (320, 512, True)]][t]):
                 y = sb.tile([P, c1 - c0], F32, name=f"y{t}{i}")

@@ -21,6 +21,7 @@ PACK = 4
 HALF = N // 2
 LIST_COLS = N // 16
 ROW0 = 16
+S_QUERIES = 80
 
 
 def tile_attend_wts_topk_kernel(tc, qT, k_words, k_scales, offs, out):
@@ -48,11 +49,11 @@ def tile_attend_wts_topk_kernel(tc, qT, k_words, k_scales, offs, out):
         nc.sync.dma_start(q_raw[0, 2][:], q_rows[:, 2:PACK, 0:P])
         nc.sync.dma_start(q_raw[1, 0][:], q_rows[:, :, P:NQ])
 
-        def cast(t, j):
+        def cast(copy, t, j, w0=0, w1=P):
             raw = q_raw[t, j]
-            nc.scalar.copy(
-                q_bf[t][:, :, j : j + raw.shape[1]].rearrange("p (c i) j -> p c j i", i=4),
-                raw[:].rearrange("p j (c i) -> p c j i", i=4),
+            copy(
+                q_bf[t][:, w0:w1, j : j + raw.shape[1]].rearrange("p (c i) j -> p c j i", i=4),
+                raw[:, :, w0:w1].rearrange("p j (c i) -> p c j i", i=4),
             )
 
         def quantize(t):
@@ -62,7 +63,7 @@ def tile_attend_wts_topk_kernel(tc, qT, k_words, k_scales, offs, out):
                 in_=q_bf[t][:].rearrange("p w j -> p (w j)"),
             )
 
-        cast(0, 0)
+        cast(nc.scalar.copy, 0, 0)
         picked_scales = sb.tile([P, N], U8, name="picked_scales", align_bytes=64)
         nc.vector.tensor_copy(picked_scales[:], pool_scales[:].indirect(offsets[:]))
         key_scales = sb.tile([P, N], U8, name="key_scales", tag="q_raw00", align_bytes=64)
@@ -70,12 +71,13 @@ def tile_attend_wts_topk_kernel(tc, qT, k_words, k_scales, offs, out):
         for r in range(4):
             queue = nc.scalar if r % 2 else nc.sync
             queue.dma_start(key_scales[:].bitcast(I32)[r:P:32, :], picked_scales[:].bitcast(I32)[ROW0 + r : 32 : 4, :])
-        cast(0, 2)
-        cast(1, 0)
+        cast(nc.scalar.copy, 0, 2)
+        cast(nc.scalar.copy, 1, 0, 0, S_QUERIES)
 
         key_words = sb.tile([P, N], U32, name="key_words", align_bytes=64)
         nc.vector.tensor_copy(key_words[:], pool_words[:].bitcast(U32).indirect(offsets[:]))
         quantize(0)
+        cast(nc.vector.tensor_copy, 1, 0, S_QUERIES, P)
         quantize(1)
 
         banks = [psum.tile([P, N], F32, name=f"bank{t}") for t in range(2)]

@@ -21,7 +21,6 @@ PACK = 4
 HALF = N // 2
 LIST_COLS = N // 16
 ROW0 = 16
-S_QUERIES = 80
 
 
 def tile_attend_wts_topk_kernel(tc, qT, k_words, k_scales, offs, out):
@@ -36,7 +35,7 @@ def tile_attend_wts_topk_kernel(tc, qT, k_words, k_scales, offs, out):
         q_rows = qT[0].rearrange("(p j) w -> p j w", j=PACK)
         words_hbm = k_words[0].rearrange("p t r -> p (t r)").bitcast(I32)
         q_raw = {(t, j): sb.tile([P, n, P], F32, name=f"q_raw{t}{j}", tag=f"q_raw{t}{j}", align_bytes=64) for t, j, n in ((0, 0, 2), (0, 2, 2), (1, 0, PACK))}
-        q_bf = [sb.tile([P, P, PACK], BF16, name=f"q_bf{t}", align_bytes=64) for t in range(2)]
+        q_bf0 = sb.tile([P, P, PACK], BF16, name="q_bf0", align_bytes=64)
         q_codes = [sb.tile([P, P], U32, name=f"q_codes{t}", align_bytes=64) for t in range(2)]
         q_scales = [sb.tile([P, P], U8, name=f"q_scales{t}", align_bytes=64) for t in range(2)]
 
@@ -49,21 +48,17 @@ def tile_attend_wts_topk_kernel(tc, qT, k_words, k_scales, offs, out):
         nc.sync.dma_start(q_raw[0, 2][:], q_rows[:, 2:PACK, 0:P])
         nc.sync.dma_start(q_raw[1, 0][:], q_rows[:, :, P:NQ])
 
-        def cast(copy, t, j, w0=0, w1=P):
-            raw = q_raw[t, j]
-            copy(
-                q_bf[t][:, w0:w1, j : j + raw.shape[1]].rearrange("p (c i) j -> p c j i", i=4),
-                raw[:, :, w0:w1].rearrange("p j (c i) -> p c j i", i=4),
-            )
+        def cast(copy, dst, raw):
+            copy(dst.rearrange("p (c i) j -> p c j i", i=4), raw.rearrange("p j (c i) -> p c j i", i=4))
 
-        def quantize(t):
+        def quantize(t, w0, w1, src):
             nc.vector.quantize_mx(
-                out=q_codes[t][:].bitcast(FP8X4),
-                scales=q_scales[t][:],
-                in_=q_bf[t][:].rearrange("p w j -> p (w j)"),
+                out=q_codes[t][:, w0:w1].bitcast(FP8X4),
+                scales=q_scales[t][:, w0:w1],
+                in_=src.rearrange("p w j -> p (w j)"),
             )
 
-        cast(nc.scalar.copy, 0, 0)
+        cast(nc.scalar.copy, q_bf0[:, :, 0:2], q_raw[0, 0][:])
         picked_scales = sb.tile([P, N], U8, name="picked_scales", align_bytes=64)
         nc.vector.tensor_copy(picked_scales[:], pool_scales[:].indirect(offsets[:]))
         key_scales = sb.tile([P, N], U8, name="key_scales", tag="q_raw00", align_bytes=64)
@@ -71,14 +66,17 @@ def tile_attend_wts_topk_kernel(tc, qT, k_words, k_scales, offs, out):
         for r in range(4):
             queue = nc.scalar if r % 2 else nc.sync
             queue.dma_start(key_scales[:].bitcast(I32)[r:P:32, :], picked_scales[:].bitcast(I32)[ROW0 + r : 32 : 4, :])
-        cast(nc.scalar.copy, 0, 2)
-        cast(nc.scalar.copy, 1, 0, 0, S_QUERIES)
+        cast(nc.scalar.copy, q_bf0[:, :, 2:PACK], q_raw[0, 2][:])
+        q_bf1a = sb.tile([P, P // 2, PACK], BF16, name="q_bf1a", align_bytes=64)
+        cast(nc.scalar.copy, q_bf1a[:], q_raw[1, 0][:, :, 0 : P // 2])
 
         key_words = sb.tile([P, N], U32, name="key_words", align_bytes=64)
         nc.vector.tensor_copy(key_words[:], pool_words[:].bitcast(U32).indirect(offsets[:]))
-        quantize(0)
-        cast(nc.vector.tensor_copy, 1, 0, S_QUERIES, P)
-        quantize(1)
+        quantize(0, 0, P, q_bf0[:])
+        q_bf1b = sb.tile([P, P // 2, PACK], BF16, name="q_bf1b", tag="q_raw02", align_bytes=64)
+        cast(nc.vector.tensor_copy, q_bf1b[:], q_raw[1, 0][:, :, P // 2 : P])
+        quantize(1, 0, P // 2, q_bf1a[:])
+        quantize(1, P // 2, P, q_bf1b[:])
 
         banks = [psum.tile([P, N], F32, name=f"bank{t}") for t in range(2)]
         neg_m = [sb.tile([P, 1], F32, name=f"neg_m{t}") for t in range(2)]

@@ -21,6 +21,8 @@ PACK = 4
 HALF = N // 2
 LIST_COLS = N // 16
 ROW0 = 16
+GROUP = 64
+Q_LOADS = ((0, GROUP), (GROUP, P), (P, NQ))
 
 
 def tile_attend_wts_topk_kernel(tc, qT, k_words, k_scales, offs, out):
@@ -34,49 +36,50 @@ def tile_attend_wts_topk_kernel(tc, qT, k_words, k_scales, offs, out):
         pool_words = sb.tile([P, T], I32, name="pool_words", align_bytes=64)
         q_rows = qT[0].rearrange("(p j) w -> p j w", j=PACK)
         words_hbm = k_words[0].rearrange("p t r -> p (t r)").bitcast(I32)
-        q_raw = {(t, j): sb.tile([P, n, P], F32, name=f"q_raw{t}{j}", tag=f"q_raw{t}{j}", align_bytes=64) for t, j, n in ((0, 0, 2), (0, 2, 2), (1, 0, PACK))}
-        q_bf0 = sb.tile([P, P, PACK], BF16, name="q_bf0", align_bytes=64)
-        q_codes = [sb.tile([P, P], U32, name=f"q_codes{t}", align_bytes=64) for t in range(2)]
-        q_scales = [sb.tile([P, P], U8, name=f"q_scales{t}", align_bytes=64) for t in range(2)]
+        q_raw = {w0: sb.tile([P, PACK, w1 - w0], F32, name=f"q_raw{w0}", tag=f"q_raw{w0}", align_bytes=64) for w0, w1 in Q_LOADS}
+        q_codes = sb.tile([P, NQ], U32, name="q_codes", align_bytes=64)
+        q_scales = sb.tile([P, NQ], U8, name="q_scales", align_bytes=64)
 
         for p0, p1 in ((0, ROW0), (32, 64), (64, P)):
             nc.vector.memset(pool_scales[:].bitcast(I32)[p0:p1, :], 0)
         nc.scalar.dma_start(pool_scales[:].bitcast(I32)[ROW0:32, :], k_scales[0].bitcast(I32))
         nc.sync.dma_start(offsets[:], offs)
-        nc.sync.dma_start(q_raw[0, 0][:], q_rows[:, 0:2, 0:P])
-        nc.sync.dma_start(pool_words[:], words_hbm)
-        nc.sync.dma_start(q_raw[0, 2][:], q_rows[:, 2:PACK, 0:P])
-        nc.sync.dma_start(q_raw[1, 0][:], q_rows[:, :, P:NQ])
+        for w0, w1 in Q_LOADS:
+            nc.sync.dma_start(q_raw[w0][:], q_rows[:, :, w0:w1])
+            if w0 == 0:
+                nc.sync.dma_start(pool_words[:], words_hbm)
 
-        def cast(copy, dst, raw):
-            copy(dst.rearrange("p (c i) j -> p c j i", i=4), raw.rearrange("p j (c i) -> p c j i", i=4))
+        def cast(copy, raw, name, tag=None):
+            q_bf = sb.tile([P, GROUP, PACK], BF16, name=name, tag=tag or name, align_bytes=64)
+            copy(q_bf[:].rearrange("p (c i) j -> p c j i", i=4), raw.rearrange("p j (c i) -> p c j i", i=4))
+            return q_bf
 
-        def quantize(t, w0, w1, src):
+        def quantize(g, q_bf):
+            cols = slice(g * GROUP, (g + 1) * GROUP)
             nc.vector.quantize_mx(
-                out=q_codes[t][:, w0:w1].bitcast(FP8X4),
-                scales=q_scales[t][:, w0:w1],
-                in_=src.rearrange("p w j -> p (w j)"),
+                out=q_codes[:, cols].bitcast(FP8X4),
+                scales=q_scales[:, cols],
+                in_=q_bf[:].rearrange("p w j -> p (w j)"),
             )
 
-        cast(nc.scalar.copy, q_bf0[:, :, 0:2], q_raw[0, 0][:])
+        q_bf0 = cast(nc.scalar.copy, q_raw[0][:], "q_bf0")
         picked_scales = sb.tile([P, N], U8, name="picked_scales", align_bytes=64)
         nc.vector.tensor_copy(picked_scales[:], pool_scales[:].indirect(offsets[:]))
-        key_scales = sb.tile([P, N], U8, name="key_scales", tag="q_raw00", align_bytes=64)
+        key_scales = sb.tile([P, N], U8, name="key_scales", tag="q_raw0", align_bytes=64)
         nc.gpsimd.memset(key_scales[:].bitcast(I32), 0)
         for r in range(4):
             queue = nc.scalar if r % 2 else nc.sync
             queue.dma_start(key_scales[:].bitcast(I32)[r:P:32, :], picked_scales[:].bitcast(I32)[ROW0 + r : 32 : 4, :])
-        cast(nc.scalar.copy, q_bf0[:, :, 2:PACK], q_raw[0, 2][:])
-        q_bf1a = sb.tile([P, P // 2, PACK], BF16, name="q_bf1a", align_bytes=64)
-        cast(nc.scalar.copy, q_bf1a[:], q_raw[1, 0][:, :, 0 : P // 2])
+        quantize(0, q_bf0)
+        q_bf1 = cast(nc.scalar.copy, q_raw[GROUP][:], "q_bf1")
+        q_bf2 = cast(nc.scalar.copy, q_raw[P][:, :, 0:GROUP], "q_bf2")
 
         key_words = sb.tile([P, N], U32, name="key_words", align_bytes=64)
         nc.vector.tensor_copy(key_words[:], pool_words[:].bitcast(U32).indirect(offsets[:]))
-        quantize(0, 0, P, q_bf0[:])
-        q_bf1b = sb.tile([P, P // 2, PACK], BF16, name="q_bf1b", tag="q_raw02", align_bytes=64)
-        cast(nc.vector.tensor_copy, q_bf1b[:], q_raw[1, 0][:, :, P // 2 : P])
-        quantize(1, 0, P // 2, q_bf1a[:])
-        quantize(1, P // 2, P, q_bf1b[:])
+        quantize(1, q_bf1)
+        q_bf3 = cast(nc.vector.tensor_copy, q_raw[P][:, :, GROUP:P], "q_bf3", tag=f"q_raw{GROUP}")
+        quantize(2, q_bf2)
+        quantize(3, q_bf3)
 
         banks = [psum.tile([P, N], F32, name=f"bank{t}") for t in range(2)]
         neg_m = [sb.tile([P, 1], F32, name=f"neg_m{t}") for t in range(2)]
@@ -84,8 +87,8 @@ def tile_attend_wts_topk_kernel(tc, qT, k_words, k_scales, offs, out):
             for c0, c1 in zip(pieces, pieces[1:]):
                 nc.tensor.matmul_mx(
                     out=banks[t][:, c0:c1],
-                    lhsT=q_codes[t][:].bitcast(FP8X4),
-                    lhsT_scale=q_scales[t][:],
+                    lhsT=q_codes[:, t * P : (t + 1) * P].bitcast(FP8X4),
+                    lhsT_scale=q_scales[:, t * P : (t + 1) * P],
                     rhs=key_words[:, c0:c1].bitcast(FP8X4),
                     rhs_scale=key_scales[:, c0:c1],
                     start=True,

@@ -44,10 +44,9 @@ def tile_attend_wts_topk_kernel(tc, qT, k_words, k_scales, offs, out):
             nc.vector.memset(pool_scales[:].bitcast(I32)[p0:p1, :], 0)
         nc.scalar.dma_start(pool_scales[:].bitcast(I32)[ROW0:32, :], k_scales[0].bitcast(I32))
         nc.sync.dma_start(offsets[:], offs)
+        nc.sync.dma_start(pool_words[:], words_hbm)
         for w0, w1 in Q_LOADS:
             nc.sync.dma_start(q_raw[w0][:], q_rows[:, :, w0:w1])
-            if w0 == 0:
-                nc.sync.dma_start(pool_words[:], words_hbm)
 
         def cast(copy, raw, name, tag=None):
             q_bf = sb.tile([P, GROUP, PACK], BF16, name=name, tag=tag or name, align_bytes=64)
@@ -62,20 +61,19 @@ def tile_attend_wts_topk_kernel(tc, qT, k_words, k_scales, offs, out):
                 in_=q_bf[:].rearrange("p w j -> p (w j)"),
             )
 
-        q_bf0 = cast(nc.scalar.copy, q_raw[0][:], "q_bf0")
         picked_scales = sb.tile([P, N], U8, name="picked_scales", align_bytes=64)
         nc.vector.tensor_copy(picked_scales[:], pool_scales[:].indirect(offsets[:]))
-        key_scales = sb.tile([P, N], U8, name="key_scales", tag="q_raw0", align_bytes=64)
-        nc.gpsimd.memset(key_scales[:].bitcast(I32), 0)
+        key_scales = sb.tile([P, N], U8, name="key_scales", align_bytes=64)
+        nc.vector.memset(key_scales[:].bitcast(I32), 0)
         for r in range(4):
-            queue = nc.scalar if r % 2 else nc.sync
-            queue.dma_start(key_scales[:].bitcast(I32)[r:P:32, :], picked_scales[:].bitcast(I32)[ROW0 + r : 32 : 4, :])
-        quantize(0, q_bf0)
+            nc.sync.dma_start(key_scales[:].bitcast(I32)[r:P:32, :], picked_scales[:].bitcast(I32)[ROW0 + r : 32 : 4, :])
+        q_bf0 = cast(nc.scalar.copy, q_raw[0][:], "q_bf0")
         q_bf1 = cast(nc.scalar.copy, q_raw[GROUP][:], "q_bf1")
         q_bf2 = cast(nc.scalar.copy, q_raw[P][:, :, 0:GROUP], "q_bf2")
 
         key_words = sb.tile([P, N], U32, name="key_words", align_bytes=64)
         nc.vector.tensor_copy(key_words[:], pool_words[:].bitcast(U32).indirect(offsets[:]))
+        quantize(0, q_bf0)
         quantize(1, q_bf1)
         q_bf3 = cast(nc.vector.tensor_copy, q_raw[P][:, :, GROUP:P], "q_bf3", tag=f"q_raw{GROUP}")
         quantize(2, q_bf2)

@@ -48,6 +48,10 @@ def tile_attend_wts_topk_kernel(tc, qT, k_words, k_scales, offs, out):
         for w0, w1 in Q_LOADS:
             nc.sync.dma_start(q_raw[w0][:], q_rows[:, :, w0:w1])
 
+        warm = sb.tile([P, 2], F32, name="warm")
+        nc.vector.memset(warm[:, 0:1], 0.0)
+        nc.scalar.activation(warm[:, 1:2], warm[:, 0:1], ACT.Exp)
+
         def cast(copy, raw, name, tag=None):
             q_bf = sb.tile([P, GROUP, PACK], BF16, name=name, tag=tag or name, align_bytes=64)
             copy(q_bf[:].rearrange("p (c i) j -> p c j i", i=4), raw.rearrange("p j (c i) -> p c j i", i=4))
@@ -66,7 +70,8 @@ def tile_attend_wts_topk_kernel(tc, qT, k_words, k_scales, offs, out):
         key_scales = sb.tile([P, N], U8, name="key_scales", align_bytes=64)
         nc.vector.memset(key_scales[:].bitcast(I32), 0)
         for r in range(4):
-            nc.sync.dma_start(key_scales[:].bitcast(I32)[r:P:32, :], picked_scales[:].bitcast(I32)[ROW0 + r : 32 : 4, :])
+            queue = nc.scalar if r % 2 else nc.sync
+            queue.dma_start(key_scales[:].bitcast(I32)[r:P:32, :], picked_scales[:].bitcast(I32)[ROW0 + r : 32 : 4, :])
         q_bf0 = cast(nc.scalar.copy, q_raw[0][:], "q_bf0")
         q_bf1 = cast(nc.scalar.copy, q_raw[GROUP][:], "q_bf1")
         q_bf2 = cast(nc.scalar.copy, q_raw[P][:, :, 0:GROUP], "q_bf2")

@@ -70,8 +70,7 @@ def tile_attend_wts_topk_kernel(tc, qT, k_words, k_scales, offs, out):
         key_scales = sb.tile([P, N], U8, name="key_scales", align_bytes=64)
         nc.vector.memset(key_scales[:].bitcast(I32), 0)
         for r in range(4):
-            queue = nc.scalar if r % 2 else nc.sync
-            queue.dma_start(key_scales[:].bitcast(I32)[r:P:32, :], picked_scales[:].bitcast(I32)[ROW0 + r : 32 : 4, :])
+            nc.scalar.dma_start(key_scales[:].bitcast(I32)[r:P:32, :], picked_scales[:].bitcast(I32)[ROW0 + r : 32 : 4, :])
         q_bf0 = cast(nc.scalar.copy, q_raw[0][:], "q_bf0")
         q_bf1 = cast(nc.scalar.copy, q_raw[GROUP][:], "q_bf1")
         q_bf2 = cast(nc.scalar.copy, q_raw[P][:, :, 0:GROUP], "q_bf2")

@@ -54,7 +54,7 @@ def tile_attend_wts_topk_kernel(tc, qT, k_words, k_scales, offs, out):
 
         def cast(copy, raw, name, tag=None):
             q_bf = sb.tile([P, GROUP, PACK], BF16, name=name, tag=tag or name, align_bytes=64)
-            copy(q_bf[:].rearrange("p (c i) j -> p c j i", i=4), raw.rearrange("p j (c i) -> p c j i", i=4))
+            copy(q_bf[:].rearrange("p (c i) j -> p c j i", i=2), raw.rearrange("p j (c i) -> p c j i", i=2))
             return q_bf
 
         def quantize(g, q_bf):

@@ -22,6 +22,7 @@ HALF = N // 2
 LIST_COLS = N // 16
 ROW0 = 16
 GROUP = 64
+LEAD = 256
 Q_LOADS = ((0, GROUP), (GROUP, P), (P, NQ))
 
 
@@ -43,8 +44,10 @@ def tile_attend_wts_topk_kernel(tc, qT, k_words, k_scales, offs, out):
         for p0, p1 in ((0, ROW0), (32, 64), (64, P)):
             nc.vector.memset(pool_scales[:].bitcast(I32)[p0:p1, :], 0)
         nc.scalar.dma_start(pool_scales[:].bitcast(I32)[ROW0:32, :], k_scales[0].bitcast(I32))
+        nc.sync.dma_start(pool_words[:, 0:LEAD], words_hbm[:, 0:LEAD])
         nc.sync.dma_start(offsets[:], offs)
-        nc.sync.dma_start(pool_words[:], words_hbm)
+        nc.sync.dma_start(pool_words[:, LEAD : 2 * LEAD], words_hbm[:, LEAD : 2 * LEAD])
+        nc.sync.dma_start(pool_words[:, 2 * LEAD : T], words_hbm[:, 2 * LEAD : T])
         for w0, w1 in Q_LOADS:
             nc.sync.dma_start(q_raw[w0][:], q_rows[:, :, w0:w1])
 

@@ -108,11 +108,18 @@ def tile_attend_wts_topk_kernel(tc, qT, k_words, k_scales, offs, out):
             rows = slice(t * P, (t + 1) * P)
             nc.scalar.activation(e[:], banks[t][:], ACT.Exp, bias=neg_m[t][:], accum_out=row_sum[:])
             nc.vector.reciprocal(inv_sum[:], row_sum[:])
-            for i, (c0, c1, on_scalar) in enumerate([[(0, 256, False), (256, 512, False)], [(0, 320, False), (320, 512, True)]][t]):
-                y = sb.tile([P, c1 - c0], F32, name=f"y{t}{i}")
-                if on_scalar:
-                    nc.scalar.activation(y[:], e[:, c0:c1], ACT.Copy, scale=inv_sum[:])
-                    nc.scalar.dma_start(out[0, rows, c0:c1], y[:])
-                else:
-                    nc.vector.tensor_scalar(y[:], e[:, c0:c1], inv_sum[:], None, ALU.mult)
-                    nc.sync.dma_start(out[0, rows, c0:c1], y[:])
+            if t == 0:
+                y_a = sb.tile([P, HALF], F32, name="y0a")
+                y_b = sb.tile([P, HALF], F32, name="y0b")
+                nc.vector.tensor_scalar(y_a[:], e[:, 0:HALF], inv_sum[:], None, ALU.mult)
+                nc.sync.dma_start(out[0, rows, 0:HALF], y_a[:])
+                nc.vector.tensor_scalar(y_b[:, 0:96], e[:, HALF : HALF + 96], inv_sum[:], None, ALU.mult)
+                nc.scalar.activation(y_b[:, 96:HALF], e[:, HALF + 96 : N], ACT.Copy, scale=inv_sum[:])
+                nc.sync.dma_start(out[0, rows, HALF:N], y_b[:])
+            else:
+                y_v = sb.tile([P, 320], F32, name="y1v")
+                y_s = sb.tile([P, N - 320], F32, name="y1s")
+                nc.vector.tensor_scalar(y_v[:], e[:, 0:320], inv_sum[:], None, ALU.mult)
+                nc.sync.dma_start(out[0, rows, 0:320], y_v[:])
+                nc.scalar.activation(y_s[:], e[:, 320:N], ACT.Copy, scale=inv_sum[:])
+                nc.scalar.dma_start(out[0, rows, 320:N], y_s[:])

@@ -23,6 +23,7 @@ LIST_COLS = N // 16
 ROW0 = 16
 GROUP = 64
 LEAD = 256
+AXI = 256
 Q_LOADS = ((0, GROUP), (GROUP, P), (P, NQ))
 
 
@@ -32,12 +33,12 @@ def tile_attend_wts_topk_kernel(tc, qT, k_words, k_scales, offs, out):
         sb = ctx.enter_context(tc.tile_pool(name="sb", bufs=1))
         psum = ctx.enter_context(tc.psum_pool(name="psum", bufs=1))
 
-        offsets = sb.tile([P, LIST_COLS], U16, name="offsets")
-        pool_scales = sb.tile([P, T], U8, name="pool_scales", align_bytes=64)
-        pool_words = sb.tile([P, T], I32, name="pool_words", align_bytes=64)
+        offsets = sb.tile([P, LIST_COLS], U16, name="offsets", align_bytes=AXI)
+        pool_scales = sb.tile([P, T], U8, name="pool_scales", align_bytes=AXI)
+        pool_words = sb.tile([P, T], I32, name="pool_words", align_bytes=AXI)
         q_rows = qT[0].rearrange("(p j) w -> p j w", j=PACK)
         words_hbm = k_words[0].rearrange("p t r -> p (t r)").bitcast(I32)
-        q_raw = {w0: sb.tile([P, PACK, w1 - w0], F32, name=f"q_raw{w0}", tag=f"q_raw{w0}", align_bytes=64) for w0, w1 in Q_LOADS}
+        q_raw = {w0: sb.tile([P, PACK, w1 - w0], F32, name=f"q_raw{w0}", tag=f"q_raw{w0}", align_bytes=AXI) for w0, w1 in Q_LOADS}
         q_codes = sb.tile([P, NQ], U32, name="q_codes", align_bytes=64)
         q_scales = sb.tile([P, NQ], U8, name="q_scales", align_bytes=64)
 
@@ -56,7 +57,7 @@ def tile_attend_wts_topk_kernel(tc, qT, k_words, k_scales, offs, out):
         nc.scalar.activation(warm[:, 1:2], warm[:, 0:1], ACT.Exp)
 
         def cast(copy, raw, name, tag=None):
-            q_bf = sb.tile([P, GROUP, PACK], BF16, name=name, tag=tag or name, align_bytes=64)
+            q_bf = sb.tile([P, GROUP, PACK], BF16, name=name, tag=tag or name, align_bytes=AXI)
             copy(q_bf[:].rearrange("p (c i) j -> p c j i", i=2), raw.rearrange("p j (c i) -> p c j i", i=2))
             return q_bf
 
@@ -68,9 +69,9 @@ def tile_attend_wts_topk_kernel(tc, qT, k_words, k_scales, offs, out):
                 in_=q_bf[:].rearrange("p w j -> p (w j)"),
             )
 
-        picked_scales = sb.tile([P, N], U8, name="picked_scales", align_bytes=64)
+        picked_scales = sb.tile([P, N], U8, name="picked_scales", align_bytes=AXI)
         nc.vector.tensor_copy(picked_scales[:], pool_scales[:].indirect(offsets[:]))
-        key_scales = sb.tile([P, N], U8, name="key_scales", align_bytes=64)
+        key_scales = sb.tile([P, N], U8, name="key_scales", align_bytes=AXI)
         nc.vector.memset(key_scales[:].bitcast(I32), 0)
         for r in range(4):
             nc.scalar.dma_start(key_scales[:].bitcast(I32)[r:P:32, :], picked_scales[:].bitcast(I32)[ROW0 + r : 32 : 4, :])
@@ -109,16 +110,16 @@ def tile_attend_wts_topk_kernel(tc, qT, k_words, k_scales, offs, out):
             nc.scalar.activation(e[:], banks[t][:], ACT.Exp, bias=neg_m[t][:], accum_out=row_sum[:])
             nc.vector.reciprocal(inv_sum[:], row_sum[:])
             if t == 0:
-                y_a = sb.tile([P, HALF], F32, name="y0a")
-                y_b = sb.tile([P, HALF], F32, name="y0b")
+                y_a = sb.tile([P, HALF], F32, name="y0a", align_bytes=AXI)
+                y_b = sb.tile([P, HALF], F32, name="y0b", align_bytes=AXI)
                 nc.vector.tensor_scalar(y_a[:], e[:, 0:HALF], inv_sum[:], None, ALU.mult)
                 nc.sync.dma_start(out[0, rows, 0:HALF], y_a[:])
                 nc.vector.tensor_scalar(y_b[:, 0:96], e[:, HALF : HALF + 96], inv_sum[:], None, ALU.mult)
                 nc.scalar.activation(y_b[:, 96:HALF], e[:, HALF + 96 : N], ACT.Copy, scale=inv_sum[:])
                 nc.sync.dma_start(out[0, rows, HALF:N], y_b[:])
             else:
-                y_v = sb.tile([P, 320], F32, name="y1v")
-                y_s = sb.tile([P, N - 320], F32, name="y1s")
+                y_v = sb.tile([P, 320], F32, name="y1v", align_bytes=AXI)
+                y_s = sb.tile([P, N - 320], F32, name="y1s", align_bytes=AXI)
                 nc.vector.tensor_scalar(y_v[:], e[:, 0:320], inv_sum[:], None, ALU.mult)
                 nc.sync.dma_start(out[0, rows, 0:320], y_v[:])
                 nc.scalar.activation(y_s[:], e[:, 320:N], ACT.Copy, scale=inv_sum[:])

@@ -24,7 +24,8 @@ ROW0 = 16
 GROUP = 64
 LEAD = 256
 AXI = 256
-Q_LOADS = ((0, GROUP), (GROUP, P), (P, NQ))
+Q_LOADS = ((0, P), (P, P + GROUP), (P + GROUP, NQ))
+S_SHARE = 16
 
 
 def tile_attend_wts_topk_kernel(tc, qT, k_words, k_scales, offs, out):
@@ -75,15 +76,20 @@ def tile_attend_wts_topk_kernel(tc, qT, k_words, k_scales, offs, out):
         nc.vector.memset(key_scales[:].bitcast(I32), 0)
         for r in range(4):
             nc.scalar.dma_start(key_scales[:].bitcast(I32)[r:P:32, :], picked_scales[:].bitcast(I32)[ROW0 + r : 32 : 4, :])
-        q_bf0 = cast(nc.scalar.copy, q_raw[0][:], "q_bf0")
-        q_bf1 = cast(nc.scalar.copy, q_raw[GROUP][:], "q_bf1")
-        q_bf2 = cast(nc.scalar.copy, q_raw[P][:, :, 0:GROUP], "q_bf2")
+        q_bf0 = cast(nc.scalar.copy, q_raw[0][:, :, 0:GROUP], "q_bf0")
+        q_bf1 = sb.tile([P, GROUP, PACK], BF16, name="q_bf1", align_bytes=AXI)
+        nc.scalar.copy(
+            q_bf1[:, 0:S_SHARE, :].rearrange("p (c i) j -> p c j i", i=2),
+            q_raw[0][:, :, GROUP : GROUP + S_SHARE].rearrange("p j (c i) -> p c j i", i=2),
+        )
+        nc.gpsimd.tensor_copy(q_bf1[:, S_SHARE:GROUP, :], q_raw[0][:, :, GROUP + S_SHARE : P].rearrange("p j w -> p w j"))
+        q_bf2 = cast(nc.scalar.copy, q_raw[P][:], "q_bf2")
 
         key_words = sb.tile([P, N], U32, name="key_words", align_bytes=64)
         nc.vector.tensor_copy(key_words[:], pool_words[:].bitcast(U32).indirect(offsets[:]))
         quantize(0, q_bf0)
         quantize(1, q_bf1)
-        q_bf3 = cast(nc.vector.tensor_copy, q_raw[P][:, :, GROUP:P], "q_bf3", tag=f"q_raw{GROUP}")
+        q_bf3 = cast(nc.vector.tensor_copy, q_raw[P + GROUP][:], "q_bf3", tag="q_raw0")
         quantize(2, q_bf2)
         quantize(3, q_bf3)
 

from contextlib import ExitStack

import concourse.mybir as mybir

NQ, D, T, N = 256, 512, 2048, 512
FLOPS = 2 * NQ * D * N

F32 = mybir.dt.float32
BF16 = mybir.dt.bfloat16
I32 = mybir.dt.int32
U32 = mybir.dt.uint32
U16 = mybir.dt.uint16
U8 = mybir.dt.uint8
FP8X4 = mybir.dt.float8_e4m3fn_x4
ALU = mybir.AluOpType
ACT = mybir.ActivationFunctionType
AXIS = mybir.AxisListType

P = 128
PACK = 4
HALF = N // 2
LIST_COLS = N // 16
ROW0 = 16
GROUP = 64
LEAD = 256
AXI = 256
Q_LOADS = ((0, P), (P, P + GROUP), (P + GROUP, NQ))
S_SHARE = 16


def tile_attend_wts_topk_kernel(tc, qT, k_words, k_scales, offs, out):
    nc = tc.nc
    with ExitStack() as ctx:
        sb = ctx.enter_context(tc.tile_pool(name="sb", bufs=1))
        psum = ctx.enter_context(tc.psum_pool(name="psum", bufs=1))

        offsets = sb.tile([P, LIST_COLS], U16, name="offsets", align_bytes=AXI)
        pool_scales = sb.tile([P, T], U8, name="pool_scales", align_bytes=AXI)
        pool_words = sb.tile([P, T], I32, name="pool_words", align_bytes=AXI)
        q_rows = qT[0].rearrange("(p j) w -> p j w", j=PACK)
        words_hbm = k_words[0].rearrange("p t r -> p (t r)").bitcast(I32)
        q_raw = {w0: sb.tile([P, PACK, w1 - w0], F32, name=f"q_raw{w0}", tag=f"q_raw{w0}", align_bytes=AXI) for w0, w1 in Q_LOADS}
        q_codes = sb.tile([P, NQ], U32, name="q_codes", align_bytes=64)
        q_scales = sb.tile([P, NQ], U8, name="q_scales", align_bytes=64)

        for p0, p1 in ((0, ROW0), (32, 64), (64, P)):
            nc.vector.memset(pool_scales[:].bitcast(I32)[p0:p1, :], 0)
        nc.scalar.dma_start(pool_scales[:].bitcast(I32)[ROW0:32, :], k_scales[0].bitcast(I32))
        nc.sync.dma_start(pool_words[:, 0:LEAD], words_hbm[:, 0:LEAD])
        nc.sync.dma_start(offsets[:], offs)
        nc.sync.dma_start(pool_words[:, LEAD : 2 * LEAD], words_hbm[:, LEAD : 2 * LEAD])
        nc.sync.dma_start(pool_words[:, 2 * LEAD : T], words_hbm[:, 2 * LEAD : T])
        for w0, w1 in Q_LOADS:
            nc.sync.dma_start(q_raw[w0][:], q_rows[:, :, w0:w1])

        warm = sb.tile([P, 2], F32, name="warm")
        nc.vector.memset(warm[:, 0:1], 0.0)
        nc.scalar.activation(warm[:, 1:2], warm[:, 0:1], ACT.Exp)

        def cast(copy, raw, name, tag=None):
            q_bf = sb.tile([P, GROUP, PACK], BF16, name=name, tag=tag or name, align_bytes=AXI)
            copy(q_bf[:].rearrange("p (c i) j -> p c j i", i=2), raw.rearrange("p j (c i) -> p c j i", i=2))
            return q_bf

        def quantize(g, q_bf):
            cols = slice(g * GROUP, (g + 1) * GROUP)
            nc.vector.quantize_mx(
                out=q_codes[:, cols].bitcast(FP8X4),
                scales=q_scales[:, cols],
                in_=q_bf[:].rearrange("p w j -> p (w j)"),
            )

        picked_scales = sb.tile([P, N], U8, name="picked_scales", align_bytes=AXI)
        nc.vector.tensor_copy(picked_scales[:], pool_scales[:].indirect(offsets[:]))
        key_scales = sb.tile([P, N], U8, name="key_scales", align_bytes=AXI)
        nc.vector.memset(key_scales[:].bitcast(I32), 0)
        for r in range(4):
            nc.scalar.dma_start(key_scales[:].bitcast(I32)[r:P:32, :], picked_scales[:].bitcast(I32)[ROW0 + r : 32 : 4, :])
        q_bf0 = cast(nc.scalar.copy, q_raw[0][:, :, 0:GROUP], "q_bf0")
        q_bf1 = sb.tile([P, GROUP, PACK], BF16, name="q_bf1", align_bytes=AXI)
        nc.scalar.copy(
            q_bf1[:, 0:S_SHARE, :].rearrange("p (c i) j -> p c j i", i=2),
            q_raw[0][:, :, GROUP : GROUP + S_SHARE].rearrange("p j (c i) -> p c j i", i=2),
        )
        nc.gpsimd.tensor_copy(q_bf1[:, S_SHARE:GROUP, :], q_raw[0][:, :, GROUP + S_SHARE : P].rearrange("p j w -> p w j"))
        q_bf2 = cast(nc.scalar.copy, q_raw[P][:], "q_bf2")

        key_words = sb.tile([P, N], U32, name="key_words", align_bytes=64)
        nc.vector.tensor_copy(key_words[:], pool_words[:].bitcast(U32).indirect(offsets[:]))
        quantize(0, q_bf0)
        quantize(1, q_bf1)
        q_bf3 = cast(nc.vector.tensor_copy, q_raw[P + GROUP][:], "q_bf3", tag="q_raw0")
        quantize(2, q_bf2)
        quantize(3, q_bf3)

        banks = [psum.tile([P, N], F32, name=f"bank{t}") for t in range(2)]
        neg_m = [sb.tile([P, 1], F32, name=f"neg_m{t}") for t in range(2)]
        for t, pieces in enumerate(((0, N), (0, N))):
            for c0, c1 in zip(pieces, pieces[1:]):
                nc.tensor.matmul_mx(
                    out=banks[t][:, c0:c1],
                    lhsT=q_codes[:, t * P : (t + 1) * P].bitcast(FP8X4),
                    lhsT_scale=q_scales[:, t * P : (t + 1) * P],
                    rhs=key_words[:, c0:c1].bitcast(FP8X4),
                    rhs_scale=key_scales[:, c0:c1],
                    start=True,
                    stop=True,
                )
            nc.vector.tensor_reduce(neg_m[t][:], banks[t][:], AXIS.X, ALU.max, negate=True)

        for t in range(2):
            e = sb.tile([P, N], F32, name=f"e{t}")
            row_sum = sb.tile([P, 1], F32, name=f"row_sum{t}")
            inv_sum = sb.tile([P, 1], F32, name=f"inv_sum{t}")
            rows = slice(t * P, (t + 1) * P)
            nc.scalar.activation(e[:], banks[t][:], ACT.Exp, bias=neg_m[t][:], accum_out=row_sum[:])
            nc.vector.reciprocal(inv_sum[:], row_sum[:])
            if t == 0:
                y_a = sb.tile([P, HALF], F32, name="y0a", align_bytes=AXI)
                y_b = sb.tile([P, HALF], F32, name="y0b", align_bytes=AXI)
                nc.vector.tensor_scalar(y_a[:], e[:, 0:HALF], inv_sum[:], None, ALU.mult)
                nc.sync.dma_start(out[0, rows, 0:HALF], y_a[:])
                nc.vector.tensor_scalar(y_b[:, 0:96], e[:, HALF : HALF + 96], inv_sum[:], None, ALU.mult)
                nc.scalar.activation(y_b[:, 96:HALF], e[:, HALF + 96 : N], ACT.Copy, scale=inv_sum[:])
                nc.sync.dma_start(out[0, rows, HALF:N], y_b[:])
            else:
                y_v = sb.tile([P, 320], F32, name="y1v", align_bytes=AXI)
                y_s = sb.tile([P, N - 320], F32, name="y1s", align_bytes=AXI)
                nc.vector.tensor_scalar(y_v[:], e[:, 0:320], inv_sum[:], None, ALU.mult)
                nc.sync.dma_start(out[0, rows, 0:320], y_v[:])
                nc.scalar.activation(y_s[:], e[:, 320:N], ACT.Copy, scale=inv_sum[:])
                nc.scalar.dma_start(out[0, rows, 320:N], y_s[:])
